import numpy as np
import ml_dtypes


def mxq(x, axis, fmt="e4m3"):
    dtype, down = {"e4m3": (ml_dtypes.float8_e4m3fn, 7), "e5m2": (ml_dtypes.float8_e5m2, 14)}[fmt]
    v = np.moveaxis(np.asarray(x, np.float32).astype(ml_dtypes.bfloat16).astype(np.float64), axis, -1)
    blocks = v.reshape(v.shape[:-1] + (-1, 32))
    amax = np.abs(blocks).max(-1, keepdims=True)
    byte = np.maximum(np.where(amax > 0, np.frexp(amax)[1] - 1 + 127, 0) - down, 1)
    scale = np.exp2(byte - 127.0)
    codes = (blocks / scale).astype(np.float32).astype(dtype).astype(np.float64)
    return np.moveaxis((codes * scale).reshape(v.shape), -1, axis)


WIDE = False


def mx_kscale(k):
    if not WIDE:
        return np.ones(k)
    levels = np.array([10, -10, 5, -5, 0])
    if k % 512:
        return np.exp2(np.random.permutation(np.resize(levels, k // 32))).repeat(32)
    a = np.empty((k // 512, 16))
    for p in range(k // 512):
        a[p, :8] = np.random.permutation(np.resize(levels, 8))
        for g in range(8):
            far = levels[np.abs(levels - a[p, g]) >= 10]
            a[p, g + 8] = far[np.random.randint(len(far))]
    return np.exp2(a.ravel()).repeat(32)


def f64(x):
    return np.asarray(x).astype(np.float64)


def striped(idx):
    return np.tile(idx.reshape(-1, 16).T, (8, 1)).astype(np.uint16)


def unstriped(offs):
    return offs[:16].T.reshape(-1).astype(np.int64)


def striped8(idx):
    return np.concatenate([x.reshape(-1, 16).T for x in idx]).astype(np.uint16)


def runs(offs, k):
    lists = np.stack([offs[16 * r : 16 * r + 16].T.reshape(-1) for r in range(8)]).astype(np.int64)
    return lists[np.arange(k) % 512 // 64]


def pack_weight(w):
    k, n = w.shape
    w = f64(np.asarray(w, np.float32).astype(ml_dtypes.bfloat16)).reshape(k // 32, 32, n)
    amax = np.abs(w).max(1)
    byte = np.clip(np.where(amax > 0, np.frexp(amax)[1] - 1 + 127 - 7, 1), 1, 254)
    scaled = (w * np.exp2(127.0 - byte)[:, None, :]).reshape(k, n).astype(np.float32)
    words = np.ascontiguousarray(scaled.reshape(k // 512, 128, 4, n).transpose(0, 1, 3, 2)).astype(ml_dtypes.float8_e4m3fn).view(np.uint8)
    return words, np.ascontiguousarray(byte.astype(np.uint8).reshape(k // 512, 16, n))


def unpack_weight(words, scales):
    g, p, n, _ = words.shape
    vals = np.ascontiguousarray(words).view(ml_dtypes.float8_e4m3fn).astype(np.float64) * np.repeat(np.exp2(scales.astype(np.float64) - 127.0), 8, axis=1)[..., None]
    return vals.transpose(0, 1, 3, 2).reshape(g * 512, n)


def relu(v):
    return np.maximum(v, 0.0)


K, T, S, H, G, U = 512, 2048, 512, 512, 2048, 1024


def setup_inputs():
    n = np.random.standard_normal
    s = mx_kscale(K)[:, None]
    packed_xT = pack_weight(n((K, T)) * s)
    packed_dT = pack_weight(n((K, G)) / s)
    return {
        "x_words": packed_xT[0],
        "x_scales": packed_xT[1],
        "w1": (n((K, H)) / np.sqrt(K) / s).astype(np.float32),
        "gs": (np.random.uniform(0.5, 1.5, (K, 1)) * s).astype(np.float32),
        "d_words": packed_dT[0],
        "d_scales": packed_dT[1],
        "mem": n((H, U)).astype(np.float32),
        "offs": striped(np.random.permutation(T)[:S]),
        "n1": striped8(np.stack([np.random.permutation(S) for _ in range(8)])),
        "n2": striped8(np.stack([np.random.permutation(S) for _ in range(8)])),
        "k1": striped8(np.random.randint(0, G, (8, H))),
        "n3": striped8(np.stack([np.random.permutation(U)[:S] for _ in range(8)])),
    }


def reference(x_words, x_scales, w1, gs, d_words, d_scales, mem, offs, n1, n2, k1, n3):
    d_k1 = unpack_weight(d_words, d_scales)[np.arange(K)[:, None], runs(k1, K)]
    xq = unpack_weight(x_words, x_scales)[:, unstriped(offs)]
    y = mxq(f64(w1), 0, "e4m3").T @ xq
    pa = y - (y[np.arange(H)[:, None], runs(n1, H)])
    pb = y[np.arange(H)[:, None], runs(n2, H)] - y
    z = f64(gs) * (relu(np.minimum(pa, pb)) - (relu(-1.0 * np.maximum(pa, pb))))
    h = 0.0625 * ((d_k1.T @ mxq(z, 0, "e4m3")))
    out = f64(mem).copy()
    out[np.arange(H)[:, None], runs(n3, H)] = h
    return out

@@ -1,0 +1,206 @@
+from contextlib import ExitStack
+
+import concourse.mybir as mybir
+
+K, T, S, H, G, U = 512, 2048, 512, 512, 2048, 1024
+FLOPS = 2 * K * H * S + 2 * K * H * S
+
+F32 = mybir.dt.float32
+BF16 = mybir.dt.bfloat16
+I32 = mybir.dt.int32
+U32 = mybir.dt.uint32
+U16 = mybir.dt.uint16
+U8 = mybir.dt.uint8
+FP8X4 = mybir.dt.float8_e4m3fn_x4
+ALU = mybir.AluOpType
+ACT = mybir.ActivationFunctionType
+
+P = 128
+PACK = 4
+HALF = S // 2
+LIST_COLS = S // 16
+HALF_COLS = LIST_COLS // 2
+
+
+def tile_picked_denseminmodpage_none_p_kernel(
+    tc, x_words, x_scales, w1, gs, d_words, d_scales, mem, offs, n1, n2, k1, n3, out
+):
+    nc = tc.nc
+    with ExitStack() as ctx:
+        lists = ctx.enter_context(tc.tile_pool(name="lists", bufs=1))
+        sb = ctx.enter_context(tc.tile_pool(name="sb", bufs=1))
+        psum = ctx.enter_context(tc.psum_pool(name="psum", bufs=8))
+
+        def tile(name, shape, dtype, tag=None):
+            return sb.tile(shape, dtype, name=name, tag=tag or name, align_bytes=64)
+
+        def load_list(name, src):
+            dst = lists.tile([P, LIST_COLS], U16, name=name)
+            nc.sync.dma_start(dst[:], src)
+            return dst
+
+        def half(lst, h):
+            return lst[:, h * HALF_COLS : (h + 1) * HALF_COLS]
+
+        def cols(h):
+            return slice(h * HALF, (h + 1) * HALF)
+
+        xs_table = tile("xs_table", [P, T], U8)
+        ds_table = tile("ds_table", [P, G], U8)
+        d_plane = tile("d_plane", [P, H], U8)
+        nc.vector.memset(xs_table[:].bitcast(I32), 0)
+        nc.gpsimd.memset(ds_table[:].bitcast(I32), 0)
+        nc.gpsimd.memset(d_plane[:].bitcast(I32), 0)
+        for q in range(4):
+            nc.scalar.dma_start(xs_table[32 * q : 32 * q + 4, :].bitcast(I32), x_scales[0, 4 * q : 4 * q + 4, :].bitcast(I32))
+
+        w_rows = w1.rearrange("(p j) c -> p j c", j=PACK)
+        w_raw = []
+        for c in range(2):
+            raw = tile("w_raw%d" % c, [P, PACK, H // 2], F32)
+            nc.sync.dma_start(raw[:], w_rows[:, :, c * (H // 2) : (c + 1) * (H // 2)])
+            w_raw.append(raw)
+        offs_t = load_list("offs_t", offs)
+        x_table = tile("x_table", [P, T], U32)
+        nc.sync.dma_start(x_table[:].bitcast(I32), x_words[0].rearrange("p n r -> p (n r)").bitcast(I32))
+        gain = tile("gain", [P, PACK], F32)
+        nc.sync.dma_start(gain[:], gs.rearrange("(p t) o -> p (t o)", t=PACK))
+        k1_t = load_list("k1_t", k1)
+        for i in range(2):
+            nc.sync.dma_start(ds_table[i:P:16, :].bitcast(I32), d_scales[0, i:16:2, :].bitcast(I32))
+        n2_t = load_list("n2_t", n2)
+        n1_t = load_list("n1_t", n1)
+        d_table = tile("d_table", [P, G], U32)
+        nc.sync.dma_start(d_table[:].bitcast(I32), d_words[0].rearrange("p n r -> p (n r)").bitcast(I32))
+        n3_t = load_list("n3_t", n3)
+        mem_rows = mem.rearrange("(p t) u -> t p u", t=PACK)
+        out_rows = out.rearrange("(p t) u -> t p u", t=PACK)
+        page = []
+        for t in range(PACK):
+            page.append(tile("page%d" % t, [P, U], F32))
+            nc.sync.dma_start(page[t][:], mem_rows[t])
+
+        w_bf = tile("w_bf", [P, PACK, P, PACK], BF16)
+        M2 = P // 2
+        nc.scalar.copy(w_bf[:, :, 0:M2, :], w_raw[0][:].rearrange("p j (m t) -> p t m j", t=PACK))
+        nc.vector.tensor_copy(w_bf[:, :, M2:P, :], w_raw[1][:].rearrange("p j (m t) -> p t m j", t=PACK))
+        w_codes = tile("w_codes", [P, H], U32)
+        w_plane = tile("w_plane", [P, H], U8)
+        nc.vector.quantize_mx(w_codes[:].bitcast(FP8X4), w_plane[:], w_bf[:].rearrange("p t m j -> p (t m j)"))
+
+        x_plane = tile("x_plane", [P, S], U8)
+        nc.vector.tensor_copy(x_plane[:], xs_table[:].indirect(offs_t[:]))
+        x_codes = tile("x_codes", [P, S], U32)
+        for h in range(2):
+            nc.vector.tensor_copy(x_codes[:, cols(h)], x_table[:].indirect(half(offs_t, h)))
+
+        ds_picked = tile("ds_picked", [P, H], U8, tag="x_table")
+        nc.vector.tensor_copy(ds_picked[:], ds_table[:].indirect(k1_t[:]))
+        ds_dealt = tile("ds_dealt", [P, H], U8)
+        nc.vector.tensor_copy(
+            ds_dealt[:].rearrange("p (t m) -> p t m", t=PACK), ds_picked[:].rearrange("p (m t) -> p t m", t=PACK)
+        )
+        for i in range(4):
+            src = 16 * (i // 2) + i % 2
+            nc.sync.dma_start(d_plane[i:P:32, :].bitcast(I32), ds_dealt[src:P:32, :].bitcast(I32))
+
+        def product(acc, codes, plane, t, rhs, rhs_plane):
+            m = slice(t * P, (t + 1) * P)
+            nc.tensor.matmul_mx(acc, lhsT=codes[:, m].bitcast(FP8X4), lhsT_scale=plane[:, m],
+                                rhs=rhs.bitcast(FP8X4), rhs_scale=rhs_plane, start=True, stop=True)
+
+        y_acc = {}
+        for h in range(2):
+            acc = psum.tile([P, HALF], F32, name="acc0%d" % h, tag="acc")
+            product(acc[:], w_codes, w_plane, 0, x_codes[:, cols(h)], x_plane[:, cols(h)])
+            y_acc[0, h] = acc[:]
+        for t in range(1, PACK):
+            acc = psum.tile([P, S], F32, name="acc%d" % t, tag="acc")
+            product(acc[:], w_codes, w_plane, t, x_codes[:], x_plane[:])
+            for h in range(2):
+                y_acc[t, h] = acc[:, cols(h)]
+            y_acc[t] = acc[:]
+
+        def scaled(dst, src, t):
+            nc.scalar.activation(dst, src, ACT.Copy, scale=gain[:, t : t + 1])
+
+        y_win = [tile("y_win%d" % t, [P, S], F32) for t in range(PACK)]
+        y_own = {}
+        for t in range(PACK):
+            y_own[t, 0] = tile("y_own%d0" % t, [P, HALF], F32)
+            if t == 0:
+                scaled(y_win[0][:, cols(0)], y_acc[0, 0], 0)
+                scaled(y_own[0, 0][:], y_acc[0, 0], 0)
+                scaled(y_win[0][:, cols(1)], y_acc[0, 1], 0)
+            else:
+                scaled(y_win[t][:], y_acc[t], t)
+                scaled(y_own[t, 0][:], y_acc[t, 0], t)
+        for t in range(PACK):
+            y_own[t, 1] = tile("y_own%d1" % t, [P, HALF], F32)
+            scaled(y_own[t, 1][:], y_acc[t, 1], t)
+
+        def differences(dst, lst, t, h):
+            nc.vector.tensor_tensor(dst[:, t, :], y_win[t][:].indirect(half(lst, h)), y_own[t, h][:], ALU.subtract)
+
+        def rounded(name, src, func, scale, tag=None):
+            dst = tile(name, [P, HALF, PACK], BF16, tag=tag)
+            nc.scalar.activation(dst[:], src[:].rearrange("p t j -> p j t"), func, scale=scale)
+            return dst[:].rearrange("p j t -> p (j t)")
+
+        def select_and_quantise(h, pa, pb, pb_pos):
+            pb_neg = tile("pb_neg%d" % h, [P, HALF * PACK], BF16)
+            nc.vector.tensor_scalar(pb_neg[:], pb, 0.0, None, ALU.min)
+            low = tile("low%d" % h, [P, HALF * PACK], BF16)
+            nc.vector.tensor_tensor(low[:], pa, pb_pos, ALU.min)
+            z = tile("z%d" % h, [P, HALF * PACK], BF16)
+            nc.vector.tensor_tensor(z[:], low[:], pb_neg[:], ALU.max)
+            codes = tile("z_codes%d" % h, [P, HALF], U32)
+            plane = tile("z_plane%d" % h, [P, HALF], U8)
+            nc.vector.quantize_mx(codes[:].bitcast(FP8X4), plane[:], z[:])
+            return codes, plane
+
+        def second_product(h, t, zq, tag=None):
+            acc = psum.tile([P, HALF], F32, name="hacc%d%d" % (h, t), tag="acc")
+            product(acc[:], d_codes, d_plane, t, zq[0][:], zq[1][:])
+            hv = tile("h%d%d" % (h, t), [P, HALF], F32, tag=tag)
+            nc.scalar.activation(hv[:], acc[:], ACT.Copy, scale=0.0625)
+            return hv
+
+        def scatter(h, t, hv):
+            nc.vector.tensor_copy(page[t][:].indirect(half(n3_t, h)), hv[:])
+
+        na0 = tile("na0", [P, PACK, HALF], F32)
+        pb0 = tile("pb0", [P, PACK, HALF], F32)
+        for t in range(PACK):
+            differences(pb0, n2_t, t, 0)
+            differences(na0, n1_t, t, 0)
+        pb1 = tile("pb1", [P, PACK, HALF], F32)
+        for t in range(PACK):
+            differences(pb1, n2_t, t, 1)
+        b0 = rounded("b0", pb0, ACT.Copy, 1.0)
+        r0 = rounded("r0", pb0, ACT.Relu, 1.0)
+        a0 = rounded("a0", na0, ACT.Copy, -1.0)
+
+        d_picked = tile("d_picked", [P, H], U32, tag="y_own30")
+        nc.vector.tensor_copy(d_picked[:], d_table[:].indirect(k1_t[:]))
+        d_codes = tile("d_codes", [P, H], U32)
+        nc.vector.tensor_copy(
+            d_codes[:].rearrange("p (t m) -> p t m", t=PACK), d_picked[:].rearrange("p (m t) -> p t m", t=PACK)
+        )
+
+        zq0 = select_and_quantise(0, a0, b0, r0)
+        na1 = tile("na1", [P, PACK, HALF], F32, tag="a0")
+        for t in range(PACK):
+            differences(na1, n1_t, t, 1)
+        b1 = rounded("b1", pb1, ACT.Copy, 1.0)
+        r1 = rounded("r1", pb1, ACT.Relu, 1.0)
+        h0 = [second_product(0, t, zq0) for t in range(PACK - 1)]
+        a1 = rounded("a1", na1, ACT.Copy, -1.0)
+        for t in range(PACK - 1):
+            scatter(0, t, h0[t])
+        zq1 = select_and_quantise(1, a1, b1, r1)
+        last = second_product(0, PACK - 1, zq0, tag="a1")
+        scatter(0, PACK - 1, last)
+        for t in range(PACK):
+            scatter(1, t, second_product(1, t, zq1))
+            nc.sync.dma_start(out_rows[t], page[t][:])

@@ -20,6 +20,7 @@ PACK = 4
 HALF = S // 2
 LIST_COLS = S // 16
 HALF_COLS = LIST_COLS // 2
+W_SPLIT = 48
 
 
 def tile_picked_denseminmodpage_none_p_kernel(
@@ -29,6 +30,7 @@ def tile_picked_denseminmodpage_none_p_kernel(
     with ExitStack() as ctx:
         lists = ctx.enter_context(tc.tile_pool(name="lists", bufs=1))
         sb = ctx.enter_context(tc.tile_pool(name="sb", bufs=1))
+        reuse = ctx.enter_context(tc.tile_pool(name="reuse", bufs=1))
         psum = ctx.enter_context(tc.psum_pool(name="psum", bufs=8))
 
         def tile(name, shape, dtype, tag=None):
@@ -48,42 +50,34 @@ def tile_picked_denseminmodpage_none_p_kernel(
         xs_table = tile("xs_table", [P, T], U8)
         ds_table = tile("ds_table", [P, G], U8)
         d_plane = tile("d_plane", [P, H], U8)
-        nc.vector.memset(xs_table[:].bitcast(I32), 0)
+        nc.gpsimd.memset(xs_table[:].bitcast(I32), 0)
         nc.gpsimd.memset(ds_table[:].bitcast(I32), 0)
         nc.gpsimd.memset(d_plane[:].bitcast(I32), 0)
+        gain = reuse.tile([P, 32], F32, name="gain", offset=4096 - 64, align_bytes=64)
+        nc.scalar.dma_start(gain[:, 0:PACK], gs.rearrange("(p t) o -> p (t o)", t=PACK))
         for q in range(4):
             nc.scalar.dma_start(xs_table[32 * q : 32 * q + 4, :].bitcast(I32), x_scales[0, 4 * q : 4 * q + 4, :].bitcast(I32))
 
-        w_rows = w1.rearrange("(p j) c -> p j c", j=PACK)
-        w_raw = []
-        for c in range(2):
-            raw = tile("w_raw%d" % c, [P, PACK, H // 2], F32)
-            nc.sync.dma_start(raw[:], w_rows[:, :, c * (H // 2) : (c + 1) * (H // 2)])
-            w_raw.append(raw)
         offs_t = load_list("offs_t", offs)
+        k1_t = load_list("k1_t", k1)
+        n2_t = load_list("n2_t", n2)
+        w_raw = tile("w_raw", [P, PACK, H], F32)
+        nc.sync.dma_start(w_raw[:], w1.rearrange("(p j) c -> p j c", j=PACK))
         x_table = tile("x_table", [P, T], U32)
         nc.sync.dma_start(x_table[:].bitcast(I32), x_words[0].rearrange("p n r -> p (n r)").bitcast(I32))
-        gain = tile("gain", [P, PACK], F32)
-        nc.sync.dma_start(gain[:], gs.rearrange("(p t) o -> p (t o)", t=PACK))
-        k1_t = load_list("k1_t", k1)
-        for i in range(2):
-            nc.sync.dma_start(ds_table[i:P:16, :].bitcast(I32), d_scales[0, i:16:2, :].bitcast(I32))
-        n2_t = load_list("n2_t", n2)
         n1_t = load_list("n1_t", n1)
-        d_table = tile("d_table", [P, G], U32)
-        nc.sync.dma_start(d_table[:].bitcast(I32), d_words[0].rearrange("p n r -> p (n r)").bitcast(I32))
         n3_t = load_list("n3_t", n3)
+        nc.sync.dma_start(ds_table[0:P:8, :].bitcast(I32), d_scales[0].bitcast(I32))
         mem_rows = mem.rearrange("(p t) u -> t p u", t=PACK)
         out_rows = out.rearrange("(p t) u -> t p u", t=PACK)
-        page = []
-        for t in range(PACK):
-            page.append(tile("page%d" % t, [P, U], F32))
-            nc.sync.dma_start(page[t][:], mem_rows[t])
 
         w_bf = tile("w_bf", [P, PACK, P, PACK], BF16)
-        M2 = P // 2
-        nc.scalar.copy(w_bf[:, :, 0:M2, :], w_raw[0][:].rearrange("p j (m t) -> p t m j", t=PACK))
-        nc.vector.tensor_copy(w_bf[:, :, M2:P, :], w_raw[1][:].rearrange("p j (m t) -> p t m j", t=PACK))
+        w_src = w_raw[:].rearrange("p j (m t) -> p m t j", t=PACK)
+        w_dst = w_bf[:].rearrange("p t m j -> p m t j")
+        nc.scalar.copy(w_dst[:, 0:W_SPLIT], w_src[:, 0:W_SPLIT])
+        nc.vector.tensor_copy(w_dst[:, W_SPLIT:P], w_src[:, W_SPLIT:P])
+        d_table = tile("d_table", [P, G], U32, tag="w_raw")
+        nc.sync.dma_start(d_table[:].bitcast(I32), d_words[0].rearrange("p n r -> p (n r)").bitcast(I32))
         w_codes = tile("w_codes", [P, H], U32)
         w_plane = tile("w_plane", [P, H], U8)
         nc.vector.quantize_mx(w_codes[:].bitcast(FP8X4), w_plane[:], w_bf[:].rearrange("p t m j -> p (t m j)"))
@@ -101,8 +95,12 @@ def tile_picked_denseminmodpage_none_p_kernel(
             ds_dealt[:].rearrange("p (t m) -> p t m", t=PACK), ds_picked[:].rearrange("p (m t) -> p t m", t=PACK)
         )
         for i in range(4):
-            src = 16 * (i // 2) + i % 2
-            nc.sync.dma_start(d_plane[i:P:32, :].bitcast(I32), ds_dealt[src:P:32, :].bitcast(I32))
+            nc.sync.dma_start(d_plane[i:P:32, :].bitcast(I32), ds_dealt[8 * i : P : 32, :].bitcast(I32))
+
+        page = []
+        for t, freed in enumerate(("xs_table", "w_bf", "ds_table", "x_table")):
+            page.append(tile("page%d" % t, [P, U], F32, tag=freed))
+            nc.sync.dma_start(page[t][:], mem_rows[t])
 
         def product(acc, codes, plane, t, rhs, rhs_plane):
             m = slice(t * P, (t + 1) * P)
@@ -125,22 +123,16 @@ def tile_picked_denseminmodpage_none_p_kernel(
             nc.scalar.activation(dst, src, ACT.Copy, scale=gain[:, t : t + 1])
 
         y_win = [tile("y_win%d" % t, [P, S], F32) for t in range(PACK)]
-        y_own = {}
-        for t in range(PACK):
-            y_own[t, 0] = tile("y_own%d0" % t, [P, HALF], F32)
-            if t == 0:
-                scaled(y_win[0][:, cols(0)], y_acc[0, 0], 0)
-                scaled(y_own[0, 0][:], y_acc[0, 0], 0)
-                scaled(y_win[0][:, cols(1)], y_acc[0, 1], 0)
-            else:
-                scaled(y_win[t][:], y_acc[t], t)
-                scaled(y_own[t, 0][:], y_acc[t, 0], t)
-        for t in range(PACK):
-            y_own[t, 1] = tile("y_own%d1" % t, [P, HALF], F32)
-            scaled(y_own[t, 1][:], y_acc[t, 1], t)
+        y_own = [tile("y_own%d" % t, [P, S], F32) for t in range(PACK)]
+        for h in range(2):
+            scaled(y_win[0][:, cols(h)], y_acc[0, h], 0)
+            scaled(y_own[0][:, cols(h)], y_acc[0, h], 0)
+        for t in range(1, PACK):
+            scaled(y_win[t][:], y_acc[t], t)
+            scaled(y_own[t][:], y_acc[t], t)
 
         def differences(dst, lst, t, h):
-            nc.vector.tensor_tensor(dst[:, t, :], y_win[t][:].indirect(half(lst, h)), y_own[t, h][:], ALU.subtract)
+            nc.vector.tensor_tensor(dst[:, t, :], y_win[t][:].indirect(half(lst, h)), y_own[t][:, cols(h)], ALU.subtract)
 
         def rounded(name, src, func, scale, tag=None):
             dst = tile(name, [P, HALF, PACK], BF16, tag=tag)
@@ -151,12 +143,16 @@ def tile_picked_denseminmodpage_none_p_kernel(
             pb_neg = tile("pb_neg%d" % h, [P, HALF * PACK], BF16)
             nc.vector.tensor_scalar(pb_neg[:], pb, 0.0, None, ALU.min)
             low = tile("low%d" % h, [P, HALF * PACK], BF16)
-            nc.vector.tensor_tensor(low[:], pa, pb_pos, ALU.min)
             z = tile("z%d" % h, [P, HALF * PACK], BF16)
-            nc.vector.tensor_tensor(z[:], low[:], pb_neg[:], ALU.max)
             codes = tile("z_codes%d" % h, [P, HALF], U32)
             plane = tile("z_plane%d" % h, [P, HALF], U8)
-            nc.vector.quantize_mx(codes[:].bitcast(FP8X4), plane[:], z[:])
+            parts = [slice(q * P * PACK, (q + 1) * P * PACK) for q in range(2)]
+            for c in parts:
+                nc.vector.tensor_tensor(low[:, c], pa[:, c], pb_pos[:, c], ALU.min)
+            for c in parts:
+                nc.vector.tensor_tensor(z[:, c], low[:, c], pb_neg[:, c], ALU.max)
+            for q, c in enumerate(parts):
+                nc.vector.quantize_mx(codes[:, q * P : (q + 1) * P].bitcast(FP8X4), plane[:, q * P : (q + 1) * P], z[:, c])
             return codes, plane
 
         def second_product(h, t, zq, tag=None):
@@ -169,24 +165,27 @@ def tile_picked_denseminmodpage_none_p_kernel(
         def scatter(h, t, hv):
             nc.vector.tensor_copy(page[t][:].indirect(half(n3_t, h)), hv[:])
 
-        na0 = tile("na0", [P, PACK, HALF], F32)
         pb0 = tile("pb0", [P, PACK, HALF], F32)
-        for t in range(PACK):
-            differences(pb0, n2_t, t, 0)
-            differences(na0, n1_t, t, 0)
         pb1 = tile("pb1", [P, PACK, HALF], F32)
         for t in range(PACK):
+            differences(pb0, n2_t, t, 0)
             differences(pb1, n2_t, t, 1)
+        na0 = reuse.tile([P, PACK, HALF], F32, name="na0", offset=0, align_bytes=64)
+        for t in range(PACK):
+            differences(na0, n1_t, t, 0)
         b0 = rounded("b0", pb0, ACT.Copy, 1.0)
         r0 = rounded("r0", pb0, ACT.Relu, 1.0)
         a0 = rounded("a0", na0, ACT.Copy, -1.0)
 
-        d_picked = tile("d_picked", [P, H], U32, tag="y_own30")
-        nc.vector.tensor_copy(d_picked[:], d_table[:].indirect(k1_t[:]))
+        d_picked = reuse.tile([P, H], U32, name="d_picked", offset=4096, align_bytes=64)
         d_codes = tile("d_codes", [P, H], U32)
-        nc.vector.tensor_copy(
-            d_codes[:].rearrange("p (t m) -> p t m", t=PACK), d_picked[:].rearrange("p (m t) -> p t m", t=PACK)
-        )
+        for h in range(2):
+            nc.vector.tensor_copy(d_picked[:, cols(h)], d_table[:].indirect(half(k1_t, h)))
+        for h in range(2):
+            nc.vector.tensor_copy(
+                d_codes[:].rearrange("p (t c i) -> p c t i", t=PACK, i=4)[:, h * 16 : (h + 1) * 16],
+                d_picked[:, cols(h)].rearrange("p (c i t) -> p c t i", t=PACK, i=4),
+            )
 
         zq0 = select_and_quantise(0, a0, b0, r0)
         na1 = tile("na1", [P, PACK, HALF], F32, tag="a0")

@@ -20,7 +20,7 @@ PACK = 4
 HALF = S // 2
 LIST_COLS = S // 16
 HALF_COLS = LIST_COLS // 2
-W_SPLIT = 48
+XS_SPLIT = 1408
 
 
 def tile_picked_denseminmodpage_none_p_kernel(
@@ -50,33 +50,34 @@ def tile_picked_denseminmodpage_none_p_kernel(
         xs_table = tile("xs_table", [P, T], U8)
         ds_table = tile("ds_table", [P, G], U8)
         d_plane = tile("d_plane", [P, H], U8)
-        nc.gpsimd.memset(xs_table[:].bitcast(I32), 0)
-        nc.gpsimd.memset(ds_table[:].bitcast(I32), 0)
+        for table in (xs_table, ds_table):
+            nc.vector.memset(table[:, 0:XS_SPLIT].bitcast(I32), 0)
+            nc.gpsimd.memset(table[:, XS_SPLIT:T].bitcast(I32), 0)
         nc.gpsimd.memset(d_plane[:].bitcast(I32), 0)
-        gain = reuse.tile([P, 32], F32, name="gain", offset=4096 - 64, align_bytes=64)
-        nc.scalar.dma_start(gain[:, 0:PACK], gs.rearrange("(p t) o -> p (t o)", t=PACK))
-        for q in range(4):
-            nc.scalar.dma_start(xs_table[32 * q : 32 * q + 4, :].bitcast(I32), x_scales[0, 4 * q : 4 * q + 4, :].bitcast(I32))
-
         offs_t = load_list("offs_t", offs)
         k1_t = load_list("k1_t", k1)
-        n2_t = load_list("n2_t", n2)
-        w_raw = tile("w_raw", [P, PACK, H], F32)
-        nc.sync.dma_start(w_raw[:], w1.rearrange("(p j) c -> p j c", j=PACK))
+        w_rows = w1.rearrange("(p j) c -> p j c", j=PACK)
+        w_raw = [tile("w_raw%d" % h, [P, PACK, HALF], F32) for h in range(2)]
+        nc.sync.dma_start(w_raw[0][:], w_rows[:, :, cols(0)])
+        for q in range(4):
+            nc.sync.dma_start(xs_table[32 * q : 32 * q + 4, :].bitcast(I32), x_scales[0, 4 * q : 4 * q + 4, :].bitcast(I32))
+        nc.sync.dma_start(ds_table[0:P:8, :].bitcast(I32), d_scales[0].bitcast(I32))
+        nc.sync.dma_start(w_raw[1][:], w_rows[:, :, cols(1)])
         x_table = tile("x_table", [P, T], U32)
         nc.sync.dma_start(x_table[:].bitcast(I32), x_words[0].rearrange("p n r -> p (n r)").bitcast(I32))
+        gain = reuse.tile([P, 32], F32, name="gain", offset=4096 - 64, align_bytes=64)
+        nc.sync.dma_start(gain[:, 0:PACK], gs.rearrange("(p t) o -> p (t o)", t=PACK))
+        n2_t = load_list("n2_t", n2)
         n1_t = load_list("n1_t", n1)
         n3_t = load_list("n3_t", n3)
-        nc.sync.dma_start(ds_table[0:P:8, :].bitcast(I32), d_scales[0].bitcast(I32))
         mem_rows = mem.rearrange("(p t) u -> t p u", t=PACK)
         out_rows = out.rearrange("(p t) u -> t p u", t=PACK)
 
         w_bf = tile("w_bf", [P, PACK, P, PACK], BF16)
-        w_src = w_raw[:].rearrange("p j (m t) -> p m t j", t=PACK)
         w_dst = w_bf[:].rearrange("p t m j -> p m t j")
-        nc.scalar.copy(w_dst[:, 0:W_SPLIT], w_src[:, 0:W_SPLIT])
-        nc.vector.tensor_copy(w_dst[:, W_SPLIT:P], w_src[:, W_SPLIT:P])
-        d_table = tile("d_table", [P, G], U32, tag="w_raw")
+        for h in range(2):
+            nc.scalar.copy(w_dst[:, h * (P // 2) : (h + 1) * (P // 2)], w_raw[h][:].rearrange("p j (m t) -> p m t j", t=PACK))
+        d_table = tile("d_table", [P, G], U32, tag="w_raw0")
         nc.sync.dma_start(d_table[:].bitcast(I32), d_words[0].rearrange("p n r -> p (n r)").bitcast(I32))
         w_codes = tile("w_codes", [P, H], U32)
         w_plane = tile("w_plane", [P, H], U8)
@@ -88,7 +89,7 @@ def tile_picked_denseminmodpage_none_p_kernel(
         for h in range(2):
             nc.vector.tensor_copy(x_codes[:, cols(h)], x_table[:].indirect(half(offs_t, h)))
 
-        ds_picked = tile("ds_picked", [P, H], U8, tag="x_table")
+        ds_picked = tile("ds_picked", [P, H], U8)
         nc.vector.tensor_copy(ds_picked[:], ds_table[:].indirect(k1_t[:]))
         ds_dealt = tile("ds_dealt", [P, H], U8)
         nc.vector.tensor_copy(
@@ -136,12 +137,12 @@ def tile_picked_denseminmodpage_none_p_kernel(
 
         def rounded(name, src, func, scale, tag=None):
             dst = tile(name, [P, HALF, PACK], BF16, tag=tag)
-            nc.scalar.activation(dst[:], src[:].rearrange("p t j -> p j t"), func, scale=scale)
+            nc.scalar.activation(
+                dst[:].rearrange("p (c i) t -> p c t i", i=4), src[:].rearrange("p t (c i) -> p c t i", i=4), func, scale=scale
+            )
             return dst[:].rearrange("p j t -> p (j t)")
 
-        def select_and_quantise(h, pa, pb, pb_pos):
-            pb_neg = tile("pb_neg%d" % h, [P, HALF * PACK], BF16)
-            nc.vector.tensor_scalar(pb_neg[:], pb, 0.0, None, ALU.min)
+        def select_and_quantise(h, pa, pb_pos, pb_neg):
             low = tile("low%d" % h, [P, HALF * PACK], BF16)
             z = tile("z%d" % h, [P, HALF * PACK], BF16)
             codes = tile("z_codes%d" % h, [P, HALF], U32)
@@ -187,17 +188,21 @@ def tile_picked_denseminmodpage_none_p_kernel(
                 d_picked[:, cols(h)].rearrange("p (c i t) -> p c t i", t=PACK, i=4),
             )
 
-        zq0 = select_and_quantise(0, a0, b0, r0)
+        pb_neg0 = tile("pb_neg0", [P, HALF * PACK], BF16)
+        nc.vector.tensor_scalar(pb_neg0[:], b0, 0.0, None, ALU.min)
+        zq0 = select_and_quantise(0, a0, r0, pb_neg0)
         na1 = tile("na1", [P, PACK, HALF], F32, tag="a0")
         for t in range(PACK):
             differences(na1, n1_t, t, 1)
-        b1 = rounded("b1", pb1, ACT.Copy, 1.0)
+        m1 = rounded("m1", pb1, ACT.Relu, -1.0)
         r1 = rounded("r1", pb1, ACT.Relu, 1.0)
         h0 = [second_product(0, t, zq0) for t in range(PACK - 1)]
         a1 = rounded("a1", na1, ACT.Copy, -1.0)
+        pb_neg1 = tile("pb_neg1", [P, HALF * PACK], BF16)
+        nc.scalar.activation(pb_neg1[:], m1, ACT.Copy, scale=-1.0)
         for t in range(PACK - 1):
             scatter(0, t, h0[t])
-        zq1 = select_and_quantise(1, a1, b1, r1)
+        zq1 = select_and_quantise(1, a1, r1, pb_neg1)
         last = second_product(0, PACK - 1, zq0, tag="a1")
         scatter(0, PACK - 1, last)
         for t in range(PACK):

@@ -59,8 +59,8 @@ def tile_picked_denseminmodpage_none_p_kernel(
         w_rows = w1.rearrange("(p j) c -> p j c", j=PACK)
         w_raw = [tile("w_raw%d" % h, [P, PACK, HALF], F32) for h in range(2)]
         nc.sync.dma_start(w_raw[0][:], w_rows[:, :, cols(0)])
-        for q in range(4):
-            nc.sync.dma_start(xs_table[32 * q : 32 * q + 4, :].bitcast(I32), x_scales[0, 4 * q : 4 * q + 4, :].bitcast(I32))
+        for i in range(4):
+            nc.sync.dma_start(xs_table[i:P:32, :].bitcast(I32), x_scales[0, i:16:4, :].bitcast(I32))
         nc.sync.dma_start(ds_table[0:P:8, :].bitcast(I32), d_scales[0].bitcast(I32))
         nc.sync.dma_start(w_raw[1][:], w_rows[:, :, cols(1)])
         x_table = tile("x_table", [P, T], U32)

from contextlib import ExitStack

import concourse.mybir as mybir

K, T, S, H, G, U = 512, 2048, 512, 512, 2048, 1024
FLOPS = 2 * K * H * S + 2 * K * H * S

F32 = mybir.dt.float32
BF16 = mybir.dt.bfloat16
I32 = mybir.dt.int32
U32 = mybir.dt.uint32
U16 = mybir.dt.uint16
U8 = mybir.dt.uint8
FP8X4 = mybir.dt.float8_e4m3fn_x4
ALU = mybir.AluOpType
ACT = mybir.ActivationFunctionType

P = 128
PACK = 4
HALF = S // 2
LIST_COLS = S // 16
HALF_COLS = LIST_COLS // 2
XS_SPLIT = 1408


def tile_picked_denseminmodpage_none_p_kernel(
    tc, x_words, x_scales, w1, gs, d_words, d_scales, mem, offs, n1, n2, k1, n3, out
):
    nc = tc.nc
    with ExitStack() as ctx:
        lists = ctx.enter_context(tc.tile_pool(name="lists", bufs=1))
        sb = ctx.enter_context(tc.tile_pool(name="sb", bufs=1))
        reuse = ctx.enter_context(tc.tile_pool(name="reuse", bufs=1))
        psum = ctx.enter_context(tc.psum_pool(name="psum", bufs=8))

        def tile(name, shape, dtype, tag=None):
            return sb.tile(shape, dtype, name=name, tag=tag or name, align_bytes=64)

        def load_list(name, src):
            dst = lists.tile([P, LIST_COLS], U16, name=name)
            nc.sync.dma_start(dst[:], src)
            return dst

        def half(lst, h):
            return lst[:, h * HALF_COLS : (h + 1) * HALF_COLS]

        def cols(h):
            return slice(h * HALF, (h + 1) * HALF)

        xs_table = tile("xs_table", [P, T], U8)
        ds_table = tile("ds_table", [P, G], U8)
        d_plane = tile("d_plane", [P, H], U8)
        for table in (xs_table, ds_table):
            nc.vector.memset(table[:, 0:XS_SPLIT].bitcast(I32), 0)
            nc.gpsimd.memset(table[:, XS_SPLIT:T].bitcast(I32), 0)
        nc.gpsimd.memset(d_plane[:].bitcast(I32), 0)
        offs_t = load_list("offs_t", offs)
        k1_t = load_list("k1_t", k1)
        w_rows = w1.rearrange("(p j) c -> p j c", j=PACK)
        w_raw = [tile("w_raw%d" % h, [P, PACK, HALF], F32) for h in range(2)]
        nc.sync.dma_start(w_raw[0][:], w_rows[:, :, cols(0)])
        for i in range(4):
            nc.sync.dma_start(xs_table[i:P:32, :].bitcast(I32), x_scales[0, i:16:4, :].bitcast(I32))
        nc.sync.dma_start(ds_table[0:P:8, :].bitcast(I32), d_scales[0].bitcast(I32))
        nc.sync.dma_start(w_raw[1][:], w_rows[:, :, cols(1)])
        x_table = tile("x_table", [P, T], U32)
        nc.sync.dma_start(x_table[:].bitcast(I32), x_words[0].rearrange("p n r -> p (n r)").bitcast(I32))
        gain = reuse.tile([P, 32], F32, name="gain", offset=4096 - 64, align_bytes=64)
        nc.sync.dma_start(gain[:, 0:PACK], gs.rearrange("(p t) o -> p (t o)", t=PACK))
        n2_t = load_list("n2_t", n2)
        n1_t = load_list("n1_t", n1)
        n3_t = load_list("n3_t", n3)
        mem_rows = mem.rearrange("(p t) u -> t p u", t=PACK)
        out_rows = out.rearrange("(p t) u -> t p u", t=PACK)

        w_bf = tile("w_bf", [P, PACK, P, PACK], BF16)
        w_dst = w_bf[:].rearrange("p t m j -> p m t j")
        for h in range(2):
            nc.scalar.copy(w_dst[:, h * (P // 2) : (h + 1) * (P // 2)], w_raw[h][:].rearrange("p j (m t) -> p m t j", t=PACK))
        d_table = tile("d_table", [P, G], U32, tag="w_raw0")
        nc.sync.dma_start(d_table[:].bitcast(I32), d_words[0].rearrange("p n r -> p (n r)").bitcast(I32))
        w_codes = tile("w_codes", [P, H], U32)
        w_plane = tile("w_plane", [P, H], U8)
        nc.vector.quantize_mx(w_codes[:].bitcast(FP8X4), w_plane[:], w_bf[:].rearrange("p t m j -> p (t m j)"))

        x_plane = tile("x_plane", [P, S], U8)
        nc.vector.tensor_copy(x_plane[:], xs_table[:].indirect(offs_t[:]))
        x_codes = tile("x_codes", [P, S], U32)
        for h in range(2):
            nc.vector.tensor_copy(x_codes[:, cols(h)], x_table[:].indirect(half(offs_t, h)))

        ds_picked = tile("ds_picked", [P, H], U8)
        nc.vector.tensor_copy(ds_picked[:], ds_table[:].indirect(k1_t[:]))
        ds_dealt = tile("ds_dealt", [P, H], U8)
        nc.vector.tensor_copy(
            ds_dealt[:].rearrange("p (t m) -> p t m", t=PACK), ds_picked[:].rearrange("p (m t) -> p t m", t=PACK)
        )
        for i in range(4):
            nc.sync.dma_start(d_plane[i:P:32, :].bitcast(I32), ds_dealt[8 * i : P : 32, :].bitcast(I32))

        page = []
        for t, freed in enumerate(("xs_table", "w_bf", "ds_table", "x_table")):
            page.append(tile("page%d" % t, [P, U], F32, tag=freed))
            nc.sync.dma_start(page[t][:], mem_rows[t])

        def product(acc, codes, plane, t, rhs, rhs_plane):
            m = slice(t * P, (t + 1) * P)
            nc.tensor.matmul_mx(acc, lhsT=codes[:, m].bitcast(FP8X4), lhsT_scale=plane[:, m],
                                rhs=rhs.bitcast(FP8X4), rhs_scale=rhs_plane, start=True, stop=True)

        y_acc = {}
        for h in range(2):
            acc = psum.tile([P, HALF], F32, name="acc0%d" % h, tag="acc")
            product(acc[:], w_codes, w_plane, 0, x_codes[:, cols(h)], x_plane[:, cols(h)])
            y_acc[0, h] = acc[:]
        for t in range(1, PACK):
            acc = psum.tile([P, S], F32, name="acc%d" % t, tag="acc")
            product(acc[:], w_codes, w_plane, t, x_codes[:], x_plane[:])
            for h in range(2):
                y_acc[t, h] = acc[:, cols(h)]
            y_acc[t] = acc[:]

        def scaled(dst, src, t):
            nc.scalar.activation(dst, src, ACT.Copy, scale=gain[:, t : t + 1])

        y_win = [tile("y_win%d" % t, [P, S], F32) for t in range(PACK)]
        y_own = [tile("y_own%d" % t, [P, S], F32) for t in range(PACK)]
        for h in range(2):
            scaled(y_win[0][:, cols(h)], y_acc[0, h], 0)
            scaled(y_own[0][:, cols(h)], y_acc[0, h], 0)
        for t in range(1, PACK):
            scaled(y_win[t][:], y_acc[t], t)
            scaled(y_own[t][:], y_acc[t], t)

        def differences(dst, lst, t, h):
            nc.vector.tensor_tensor(dst[:, t, :], y_win[t][:].indirect(half(lst, h)), y_own[t][:, cols(h)], ALU.subtract)

        def rounded(name, src, func, scale, tag=None):
            dst = tile(name, [P, HALF, PACK], BF16, tag=tag)
            nc.scalar.activation(
                dst[:].rearrange("p (c i) t -> p c t i", i=4), src[:].rearrange("p t (c i) -> p c t i", i=4), func, scale=scale
            )
            return dst[:].rearrange("p j t -> p (j t)")

        def select_and_quantise(h, pa, pb_pos, pb_neg):
            low = tile("low%d" % h, [P, HALF * PACK], BF16)
            z = tile("z%d" % h, [P, HALF * PACK], BF16)
            codes = tile("z_codes%d" % h, [P, HALF], U32)
            plane = tile("z_plane%d" % h, [P, HALF], U8)
            parts = [slice(q * P * PACK, (q + 1) * P * PACK) for q in range(2)]
            for c in parts:
                nc.vector.tensor_tensor(low[:, c], pa[:, c], pb_pos[:, c], ALU.min)
            for c in parts:
                nc.vector.tensor_tensor(z[:, c], low[:, c], pb_neg[:, c], ALU.max)
            for q, c in enumerate(parts):
                nc.vector.quantize_mx(codes[:, q * P : (q + 1) * P].bitcast(FP8X4), plane[:, q * P : (q + 1) * P], z[:, c])
            return codes, plane

        def second_product(h, t, zq, tag=None):
            acc = psum.tile([P, HALF], F32, name="hacc%d%d" % (h, t), tag="acc")
            product(acc[:], d_codes, d_plane, t, zq[0][:], zq[1][:])
            hv = tile("h%d%d" % (h, t), [P, HALF], F32, tag=tag)
            nc.scalar.activation(hv[:], acc[:], ACT.Copy, scale=0.0625)
            return hv

        def scatter(h, t, hv):
            nc.vector.tensor_copy(page[t][:].indirect(half(n3_t, h)), hv[:])

        pb0 = tile("pb0", [P, PACK, HALF], F32)
        pb1 = tile("pb1", [P, PACK, HALF], F32)
        for t in range(PACK):
            differences(pb0, n2_t, t, 0)
            differences(pb1, n2_t, t, 1)
        na0 = reuse.tile([P, PACK, HALF], F32, name="na0", offset=0, align_bytes=64)
        for t in range(PACK):
            differences(na0, n1_t, t, 0)
        b0 = rounded("b0", pb0, ACT.Copy, 1.0)
        r0 = rounded("r0", pb0, ACT.Relu, 1.0)
        a0 = rounded("a0", na0, ACT.Copy, -1.0)

        d_picked = reuse.tile([P, H], U32, name="d_picked", offset=4096, align_bytes=64)
        d_codes = tile("d_codes", [P, H], U32)
        for h in range(2):
            nc.vector.tensor_copy(d_picked[:, cols(h)], d_table[:].indirect(half(k1_t, h)))
        for h in range(2):
            nc.vector.tensor_copy(
                d_codes[:].rearrange("p (t c i) -> p c t i", t=PACK, i=4)[:, h * 16 : (h + 1) * 16],
                d_picked[:, cols(h)].rearrange("p (c i t) -> p c t i", t=PACK, i=4),
            )

        pb_neg0 = tile("pb_neg0", [P, HALF * PACK], BF16)
        nc.vector.tensor_scalar(pb_neg0[:], b0, 0.0, None, ALU.min)
        zq0 = select_and_quantise(0, a0, r0, pb_neg0)
        na1 = tile("na1", [P, PACK, HALF], F32, tag="a0")
        for t in range(PACK):
            differences(na1, n1_t, t, 1)
        m1 = rounded("m1", pb1, ACT.Relu, -1.0)
        r1 = rounded("r1", pb1, ACT.Relu, 1.0)
        h0 = [second_product(0, t, zq0) for t in range(PACK - 1)]
        a1 = rounded("a1", na1, ACT.Copy, -1.0)
        pb_neg1 = tile("pb_neg1", [P, HALF * PACK], BF16)
        nc.scalar.activation(pb_neg1[:], m1, ACT.Copy, scale=-1.0)
        for t in range(PACK - 1):
            scatter(0, t, h0[t])
        zq1 = select_and_quantise(1, a1, r1, pb_neg1)
        last = second_product(0, PACK - 1, zq0, tag="a1")
        scatter(0, PACK - 1, last)
        for t in range(PACK):
            scatter(1, t, second_product(1, t, zq1))
            nc.sync.dma_start(out_rows[t], page[t][:])
